import numpy as np
import ml_dtypes


def mxq(x, axis, fmt="e4m3"):
    dtype, down = {"e4m3": (ml_dtypes.float8_e4m3fn, 7), "e5m2": (ml_dtypes.float8_e5m2, 14)}[fmt]
    v = np.moveaxis(np.asarray(x, np.float32).astype(ml_dtypes.bfloat16).astype(np.float64), axis, -1)
    blocks = v.reshape(v.shape[:-1] + (-1, 32))
    amax = np.abs(blocks).max(-1, keepdims=True)
    byte = np.maximum(np.where(amax > 0, np.frexp(amax)[1] - 1 + 127, 0) - down, 1)
    scale = np.exp2(byte - 127.0)
    codes = (blocks / scale).astype(np.float32).astype(dtype).astype(np.float64)
    return np.moveaxis((codes * scale).reshape(v.shape), -1, axis)


WIDE = False


def mx_kscale(k):
    if not WIDE:
        return np.ones(k)
    levels = np.array([10, -10, 5, -5, 0])
    if k % 512:
        return np.exp2(np.random.permutation(np.resize(levels, k // 32))).repeat(32)
    a = np.empty((k // 512, 16))
    for p in range(k // 512):
        a[p, :8] = np.random.permutation(np.resize(levels, 8))
        for g in range(8):
            far = levels[np.abs(levels - a[p, g]) >= 10]
            a[p, g + 8] = far[np.random.randint(len(far))]
    return np.exp2(a.ravel()).repeat(32)


def f64(x):
    return np.asarray(x).astype(np.float64)


def striped(idx):
    return np.tile(idx.reshape(-1, 16).T, (8, 1)).astype(np.uint16)


def unstriped(offs):
    return offs[:16].T.reshape(-1).astype(np.int64)


def pack_weight(w):
    k, n = w.shape
    w = f64(np.asarray(w, np.float32).astype(ml_dtypes.bfloat16)).reshape(k // 32, 32, n)
    amax = np.abs(w).max(1)
    byte = np.clip(np.where(amax > 0, np.frexp(amax)[1] - 1 + 127 - 7, 1), 1, 254)
    scaled = (w * np.exp2(127.0 - byte)[:, None, :]).reshape(k, n).astype(np.float32)
    words = np.ascontiguousarray(scaled.reshape(k // 512, 128, 4, n).transpose(0, 1, 3, 2)).astype(ml_dtypes.float8_e4m3fn).view(np.uint8)
    return words, np.ascontiguousarray(byte.astype(np.uint8).reshape(k // 512, 16, n))


def unpack_weight(words, scales):
    g, p, n, _ = words.shape
    vals = np.ascontiguousarray(words).view(ml_dtypes.float8_e4m3fn).astype(np.float64) * np.repeat(np.exp2(scales.astype(np.float64) - 127.0), 8, axis=1)[..., None]
    return vals.transpose(0, 1, 3, 2).reshape(g * 512, n)


K, T, E, C, N = 2048, 768, 6, 128, 384


def by_expert(wq, xq):
    return np.concatenate([wq[e].T @ xq[:, e * C:(e + 1) * C] for e in range(E)], axis=1)


def setup_inputs():
    n = np.random.standard_normal
    s = mx_kscale(K)[:, None]
    packed = [pack_weight(m) for m in n((E, K, N)) / np.sqrt(K) / s[None]]
    return {
        "xT": (n((K, T)) * s).astype(np.float32),
        "w_words": np.stack([m[0] for m in packed]),
        "w_scales": np.stack([m[1] for m in packed]),
        "b": (0.3 * n((N, E))).astype(np.float32),
        "gate": np.tile(np.random.uniform(0.2, 1.0, E * C), (N, 1)).astype(np.float32),
        "offs": striped(np.random.permutation(T)[:E * C]),
    }


def reference(xT, w_words, w_scales, b, gate, offs):
    idx = unstriped(offs)
    xq = mxq(f64(xT)[:, idx], 0, "e4m3")
    w = np.stack([unpack_weight(w_words[e], w_scales[e]) for e in range(E)])
    y = by_expert(w, xq)
    y = y + np.repeat(f64(b), C, axis=1)
    out = np.zeros((N, T))
    out[:, idx] = f64(gate) * y
    return out

@@ -1,0 +1,129 @@
+from contextlib import ExitStack
+
+import concourse.mybir as mybir
+
+K, T, E, C, N = 2048, 768, 6, 128, 384
+FLOPS = 2 * K * N * E * C
+BYTES = 4 * K * T + E * K * N + E * (K // 32) * N + 4 * N * E + 4 * E * C + 2 * 128 * (E * C // 16) + 4 * N * T
+
+F32 = mybir.dt.float32
+BF16 = mybir.dt.bfloat16
+I32 = mybir.dt.int32
+U32 = mybir.dt.uint32
+U16 = mybir.dt.uint16
+U8 = mybir.dt.uint8
+FP8X4 = mybir.dt.float8_e4m3fn_x4
+ADD, MULT = mybir.AluOpType.add, mybir.AluOpType.mult
+
+P = 128
+PASSES = K // 512
+BLOCKS = N // P
+SLOTS = E * C
+WINDOW = 1024
+LOADS = (((0, 256), (256, 512)), ((0, 768),), ((0, 768),), ((0, 512), (512, 256)))
+COPIES = (
+    ((0, 256, "v"), (256, 512, "s")),
+    ((0, 640, "s"), (640, 128, "v")),
+    ((0, 640, "s"), (640, 128, "v")),
+    ((0, 512, "s"), (512, 256, "v")),
+)
+QUANTS = (((0, 256), (256, 512)), ((0, 512), (512, 256)), ((0, 512), (512, 256)), ((0, 512), (512, 256)))
+
+
+def tile_routed_moe_kernel(tc, xT, w_words, w_scales, b, gate, offs, out):
+    nc = tc.nc
+    with ExitStack() as ctx:
+        keep = ctx.enter_context(tc.tile_pool(name="keep", bufs=1))
+        psum = ctx.enter_context(tc.psum_pool(name="psum", bufs=8))
+
+        x_planes = xT.rearrange("(g p t) n -> g p t n", p=P, t=4)
+        raw = {}
+        offsets = keep.tile([P, SLOTS // 16], U16, name="offsets")
+        for g in range(PASSES):
+            for c0, width in LOADS[g]:
+                tile = keep.tile([P, 4, width], F32, name=f"raw_{g}_{c0}")
+                nc.sync.dma_start(tile[:], x_planes[g, :, :, c0 : c0 + width])
+                raw[g, c0] = tile
+            if g == 0:
+                nc.sync.dma_start(offsets[:], offs)
+
+        bias = keep.tile([P, BLOCKS, E], F32, name="bias")
+        nc.scalar.dma_start(bias[:], b.rearrange("(c p) e -> p c e", p=P))
+
+        w_plane = keep.tile([P, E * PASSES, N // 4], I32, name="w_plane", align_bytes=64)
+        nc.vector.memset(w_plane[:], 0)
+        plane = keep.tile([P, WINDOW], U8, name="plane", align_bytes=64)
+        nc.gpsimd.memset(plane[:], 0)
+        codes = []
+        for g in range(PASSES):
+            tile = keep.tile([P, WINDOW], I32, name=f"codes_{g}", align_bytes=64)
+            nc.vector.memset(tile[:, T:], 0)
+            codes.append(tile)
+
+        for q in range(4):
+            nc.sync.dma_start(
+                w_plane[32 * q : 32 * q + 4, :, :],
+                w_scales[:, :, 4 * q : 4 * q + 4, :].rearrange("e a q n -> q (e a) n").bitcast(I32),
+            )
+        gates = keep.tile([P, SLOTS], F32, name="gates")
+        nc.sync.dma_start(gates[:], gate[0:P, :])
+        weights = []
+        for e in range(E):
+            tile = keep.tile([P, PASSES, N], I32, name=f"weights_{e}", align_bytes=64)
+            nc.sync.dma_start(tile[:], w_words[e].rearrange("a p n r -> p a (n r)").bitcast(I32))
+            weights.append(tile)
+
+        def source(g, c0, width):
+            for l0, lw in LOADS[g]:
+                if l0 <= c0 and c0 + width <= l0 + lw:
+                    return raw[g, l0][:, :, c0 - l0 : c0 - l0 + width]
+
+        slot_codes = []
+        for g in range(PASSES):
+            grouped = keep.tile([P, T, 4], BF16, name=f"grouped_{g}", align_bytes=64)
+            for c0, width, engine in COPIES[g]:
+                view = source(g, c0, width).rearrange("p t n -> p n t")
+                if engine == "s":
+                    nc.scalar.copy(grouped[:, c0 : c0 + width, :], view)
+                else:
+                    nc.vector.tensor_copy(grouped[:, c0 : c0 + width, :], view)
+            for c0, width in QUANTS[g]:
+                nc.vector.quantize_mx(
+                    out=codes[g][:, c0 : c0 + width].bitcast(FP8X4),
+                    scales=plane[4 * g : P, c0 : c0 + width],
+                    in_=grouped[:, c0 : c0 + width, :].rearrange("p n t -> p (n t)"),
+                )
+            tile = keep.tile([P, SLOTS], U32, name=f"slot_codes_{g}", align_bytes=64)
+            nc.vector.tensor_copy(tile[:], codes[g][:].bitcast(U32).indirect(offsets[:]))
+            slot_codes.append(tile)
+        slot_plane = keep.tile([P, SLOTS], U8, name="slot_plane", align_bytes=64)
+        nc.vector.tensor_copy(slot_plane[:], plane[:].indirect(offsets[:]))
+
+        placed = []
+        for m in range(BLOCKS):
+            tile = keep.tile([P, T], F32, name=f"placed_{m}")
+            placed.append(tile)
+        w_bytes = w_plane[:].bitcast(U8)
+        for pair in range(E // 2):
+            for m in range(BLOCKS):
+                sums = psum.tile([P, 2 * C], F32, name="sums")
+                rows = slice(m * P, (m + 1) * P)
+                y = keep.tile([P, 2 * C], F32, name=f"y_{pair}_{m}")
+                for i in range(2):
+                    e = 2 * pair + i
+                    here = slice(i * C, (i + 1) * C)
+                    slots = slice(e * C, (e + 1) * C)
+                    for g in range(PASSES):
+                        nc.tensor.matmul_mx(
+                            out=sums[:, here],
+                            lhsT=weights[e][:, g, rows].bitcast(FP8X4),
+                            lhsT_scale=w_bytes[:, e * PASSES + g, rows],
+                            rhs=slot_codes[g][:, slots].bitcast(FP8X4),
+                            rhs_scale=slot_plane[4 * g : P, slots],
+                            start=(g == 0),
+                            stop=(g == PASSES - 1),
+                        )
+                    nc.vector.scalar_tensor_tensor(y[:, here], sums[:, here], bias[:, m, e : e + 1], gates[:, slots], ADD, MULT)
+                nc.vector.tensor_copy(placed[m][:].indirect(offsets[:, 16 * pair : 16 * pair + 16]), y[:])
+        for m in range(BLOCKS):
+            nc.sync.dma_start(out[m * P : (m + 1) * P, :], placed[m][:])

@@ -22,12 +22,14 @@ SLOTS = E * C
 WINDOW = 1024
 LOADS = (((0, 256), (256, 512)), ((0, 768),), ((0, 768),), ((0, 512), (512, 256)))
 COPIES = (
-    ((0, 256, "v"), (256, 512, "s")),
+    ((0, 128, "s"), (128, 128, "v"), (256, 384, "s"), (640, 128, "v")),
     ((0, 640, "s"), (640, 128, "v")),
     ((0, 640, "s"), (640, 128, "v")),
-    ((0, 512, "s"), (512, 256, "v")),
+    ((0, 256, "s"), (256, 256, "v"), (512, 128, "s"), (640, 128, "v")),
 )
-QUANTS = (((0, 256), (256, 512)), ((0, 512), (512, 256)), ((0, 512), (512, 256)), ((0, 512), (512, 256)))
+PIECES = ((0, 384), (384, 384))
+GROUPS = ((0, 3), (3, 6))
+QUANTS = (((0, 256), (256, 512)), ((0, 512), (512, 256)), ((0, 512), (512, 256)), ((256, 256), (0, 256), (512, 256)))
 
 
 def tile_routed_moe_kernel(tc, xT, w_words, w_scales, b, gate, offs, out):
@@ -94,36 +96,41 @@ def tile_routed_moe_kernel(tc, xT, w_words, w_scales, b, gate, offs, out):
                     in_=grouped[:, c0 : c0 + width, :].rearrange("p n t -> p (n t)"),
                 )
             tile = keep.tile([P, SLOTS], U32, name=f"slot_codes_{g}", align_bytes=64)
-            nc.vector.tensor_copy(tile[:], codes[g][:].bitcast(U32).indirect(offsets[:]))
+            if g < PASSES - 1:
+                nc.vector.tensor_copy(tile[:], codes[g][:].bitcast(U32).indirect(offsets[:]))
             slot_codes.append(tile)
         slot_plane = keep.tile([P, SLOTS], U8, name="slot_plane", align_bytes=64)
-        nc.vector.tensor_copy(slot_plane[:], plane[:].indirect(offsets[:]))
+        for s0, n in PIECES:
+            here = slice(s0, s0 + n)
+            picked = offsets[:, s0 // 16 : (s0 + n) // 16]
+            nc.vector.tensor_copy(slot_codes[-1][:, here], codes[-1][:].bitcast(U32).indirect(picked))
+            nc.vector.tensor_copy(slot_plane[:, here], plane[:].indirect(picked))
 
         placed = []
         for m in range(BLOCKS):
             tile = keep.tile([P, T], F32, name=f"placed_{m}")
             placed.append(tile)
         w_bytes = w_plane[:].bitcast(U8)
-        for pair in range(E // 2):
+        for e0, e1 in GROUPS:
+            slots = slice(e0 * C, e1 * C)
+            picked = offsets[:, e0 * C // 16 : e1 * C // 16]
             for m in range(BLOCKS):
-                sums = psum.tile([P, 2 * C], F32, name="sums")
+                sums = psum.tile([P, 512], F32, name="sums")
                 rows = slice(m * P, (m + 1) * P)
-                y = keep.tile([P, 2 * C], F32, name=f"y_{pair}_{m}")
-                for i in range(2):
-                    e = 2 * pair + i
-                    here = slice(i * C, (i + 1) * C)
-                    slots = slice(e * C, (e + 1) * C)
+                y = keep.tile([P, (e1 - e0) * C], F32, name=f"y_{e0}_{m}")
+                for e in range(e0, e1):
+                    here = slice((e - e0) * C, (e - e0 + 1) * C)
                     for g in range(PASSES):
                         nc.tensor.matmul_mx(
                             out=sums[:, here],
                             lhsT=weights[e][:, g, rows].bitcast(FP8X4),
                             lhsT_scale=w_bytes[:, e * PASSES + g, rows],
-                            rhs=slot_codes[g][:, slots].bitcast(FP8X4),
-                            rhs_scale=slot_plane[4 * g : P, slots],
+                            rhs=slot_codes[g][:, e * C : (e + 1) * C].bitcast(FP8X4),
+                            rhs_scale=slot_plane[4 * g : P, e * C : (e + 1) * C],
                             start=(g == 0),
                             stop=(g == PASSES - 1),
                         )
-                    nc.vector.scalar_tensor_tensor(y[:, here], sums[:, here], bias[:, m, e : e + 1], gates[:, slots], ADD, MULT)
-                nc.vector.tensor_copy(placed[m][:].indirect(offsets[:, 16 * pair : 16 * pair + 16]), y[:])
+                    nc.scalar.activation(y[:, here], sums[:, here], mybir.ActivationFunctionType.Identity, bias=bias[:, m, e : e + 1])
+                nc.vector.tensor_tensor(placed[m][:].indirect(picked), y[:], gates[:, slots], MULT)
         for m in range(BLOCKS):
             nc.sync.dma_start(out[m * P : (m + 1) * P, :], placed[m][:])

@@ -28,7 +28,8 @@ COPIES = (
     ((0, 256, "s"), (256, 256, "v"), (512, 128, "s"), (640, 128, "v")),
 )
 PIECES = ((0, 384), (384, 384))
-GROUPS = ((0, 3), (3, 6))
+GROUPS = ((0, 1), (1, 3), (3, 5), (5, 6))
+SCALE_LOADS = ((0, 2), (2, 6))
 QUANTS = (((0, 256), (256, 512)), ((0, 512), (512, 256)), ((0, 512), (512, 256)), ((256, 256), (0, 256), (512, 256)))
 
 
@@ -52,8 +53,11 @@ def tile_routed_moe_kernel(tc, xT, w_words, w_scales, b, gate, offs, out):
         bias = keep.tile([P, BLOCKS, E], F32, name="bias")
         nc.scalar.dma_start(bias[:], b.rearrange("(c p) e -> p c e", p=P))
 
-        w_plane = keep.tile([P, E * PASSES, N // 4], I32, name="w_plane", align_bytes=64)
-        nc.vector.memset(w_plane[:], 0)
+        w_planes = []
+        for e0, e1 in SCALE_LOADS:
+            tile = keep.tile([P, (e1 - e0) * PASSES, N // 4], I32, name=f"w_plane_{e0}", align_bytes=64)
+            nc.vector.memset(tile[:], 0)
+            w_planes.append(tile)
         plane = keep.tile([P, WINDOW], U8, name="plane", align_bytes=64)
         nc.gpsimd.memset(plane[:], 0)
         codes = []
@@ -62,18 +66,22 @@ def tile_routed_moe_kernel(tc, xT, w_words, w_scales, b, gate, offs, out):
             nc.vector.memset(tile[:, T:], 0)
             codes.append(tile)
 
-        for q in range(4):
-            nc.sync.dma_start(
-                w_plane[32 * q : 32 * q + 4, :, :],
-                w_scales[:, :, 4 * q : 4 * q + 4, :].rearrange("e a q n -> q (e a) n").bitcast(I32),
-            )
         gates = keep.tile([P, SLOTS], F32, name="gates")
-        nc.sync.dma_start(gates[:], gate[0:P, :])
         weights = []
-        for e in range(E):
-            tile = keep.tile([P, PASSES, N], I32, name=f"weights_{e}", align_bytes=64)
-            nc.sync.dma_start(tile[:], w_words[e].rearrange("a p n r -> p a (n r)").bitcast(I32))
-            weights.append(tile)
+        w_bytes = []
+        for (e0, e1), tile in zip(SCALE_LOADS, w_planes):
+            for i in range(4):
+                nc.sync.dma_start(
+                    tile[i:P:32, :, :],
+                    w_scales[e0:e1].rearrange("e a (q i) n -> i q (e a) n", i=4)[i].bitcast(I32),
+                )
+            if e0 == 0:
+                nc.sync.dma_start(gates[:], gate[0:P, :])
+            for e in range(e0, e1):
+                w_bytes.append(tile[:].bitcast(U8)[:, (e - e0) * PASSES : (e - e0 + 1) * PASSES, :])
+                words = keep.tile([P, PASSES, N], I32, name=f"weights_{e}", align_bytes=64)
+                nc.sync.dma_start(words[:], w_words[e].rearrange("a p n r -> p a (n r)").bitcast(I32))
+                weights.append(words)
 
         def source(g, c0, width):
             for l0, lw in LOADS[g]:
@@ -84,11 +92,12 @@ def tile_routed_moe_kernel(tc, xT, w_words, w_scales, b, gate, offs, out):
         for g in range(PASSES):
             grouped = keep.tile([P, T, 4], BF16, name=f"grouped_{g}", align_bytes=64)
             for c0, width, engine in COPIES[g]:
-                view = source(g, c0, width).rearrange("p t n -> p n t")
+                view = source(g, c0, width).rearrange("p t (c i) -> p c t i", i=4)
+                into = grouped[:, c0 : c0 + width, :].rearrange("p (c i) t -> p c t i", i=4)
                 if engine == "s":
-                    nc.scalar.copy(grouped[:, c0 : c0 + width, :], view)
+                    nc.scalar.copy(into, view)
                 else:
-                    nc.vector.tensor_copy(grouped[:, c0 : c0 + width, :], view)
+                    nc.vector.tensor_copy(into, view)
             for c0, width in QUANTS[g]:
                 nc.vector.quantize_mx(
                     out=codes[g][:, c0 : c0 + width].bitcast(FP8X4),
@@ -110,7 +119,6 @@ def tile_routed_moe_kernel(tc, xT, w_words, w_scales, b, gate, offs, out):
         for m in range(BLOCKS):
             tile = keep.tile([P, T], F32, name=f"placed_{m}")
             placed.append(tile)
-        w_bytes = w_plane[:].bitcast(U8)
         for e0, e1 in GROUPS:
             slots = slice(e0 * C, e1 * C)
             picked = offsets[:, e0 * C // 16 : e1 * C // 16]
@@ -124,13 +132,15 @@ def tile_routed_moe_kernel(tc, xT, w_words, w_scales, b, gate, offs, out):
                         nc.tensor.matmul_mx(
                             out=sums[:, here],
                             lhsT=weights[e][:, g, rows].bitcast(FP8X4),
-                            lhsT_scale=w_bytes[:, e * PASSES + g, rows],
+                            lhsT_scale=w_bytes[e][:, g, rows],
                             rhs=slot_codes[g][:, e * C : (e + 1) * C].bitcast(FP8X4),
                             rhs_scale=slot_plane[4 * g : P, e * C : (e + 1) * C],
                             start=(g == 0),
                             stop=(g == PASSES - 1),
                         )
                     nc.scalar.activation(y[:, here], sums[:, here], mybir.ActivationFunctionType.Identity, bias=bias[:, m, e : e + 1])
-                nc.vector.tensor_tensor(placed[m][:].indirect(picked), y[:], gates[:, slots], MULT)
+                z = keep.tile([P, (e1 - e0) * C], F32, name=f"z_{e0}_{m}")
+                nc.gpsimd.tensor_tensor(z[:], y[:], gates[:, slots], MULT)
+                nc.vector.tensor_copy(placed[m][:].indirect(picked), z[:])
         for m in range(BLOCKS):
             nc.sync.dma_start(out[m * P : (m + 1) * P, :], placed[m][:])

@@ -25,12 +25,12 @@ COPIES = (
     ((0, 128, "s"), (128, 128, "v"), (256, 384, "s"), (640, 128, "v")),
     ((0, 640, "s"), (640, 128, "v")),
     ((0, 640, "s"), (640, 128, "v")),
-    ((0, 256, "s"), (256, 256, "v"), (512, 128, "s"), (640, 128, "v")),
+    ((0, 256, "s"), (256, 256, "s"), (512, 256, "v")),
 )
 PIECES = ((0, 384), (384, 384))
 GROUPS = ((0, 1), (1, 3), (3, 5), (5, 6))
-SCALE_LOADS = ((0, 2), (2, 6))
-QUANTS = (((0, 256), (256, 512)), ((0, 512), (512, 256)), ((0, 512), (512, 256)), ((256, 256), (0, 256), (512, 256)))
+SCALE_LOADS = ((0, 1), (1, 3), (3, 6))
+QUANTS = (((0, 256), (256, 512)), ((0, 512), (512, 256)), ((0, 512), (512, 256)), ((0, 256), (256, 256), (512, 256)))
 
 
 def tile_routed_moe_kernel(tc, xT, w_words, w_scales, b, gate, offs, out):
@@ -75,13 +75,13 @@ def tile_routed_moe_kernel(tc, xT, w_words, w_scales, b, gate, offs, out):
                     tile[i:P:32, :, :],
                     w_scales[e0:e1].rearrange("e a (q i) n -> i q (e a) n", i=4)[i].bitcast(I32),
                 )
-            if e0 == 0:
-                nc.sync.dma_start(gates[:], gate[0:P, :])
             for e in range(e0, e1):
                 w_bytes.append(tile[:].bitcast(U8)[:, (e - e0) * PASSES : (e - e0 + 1) * PASSES, :])
                 words = keep.tile([P, PASSES, N], I32, name=f"weights_{e}", align_bytes=64)
                 nc.sync.dma_start(words[:], w_words[e].rearrange("a p n r -> p a (n r)").bitcast(I32))
                 weights.append(words)
+                if e == 0:
+                    nc.sync.dma_start(gates[:], gate[0:P, :])
 
         def source(g, c0, width):
             for l0, lw in LOADS[g]:

@@ -3,8 +3,16 @@ from contextlib import ExitStack
 import concourse.mybir as mybir
 
 K, T, E, C, N = 2048, 768, 6, 128, 384
-FLOPS = 2 * K * N * E * C
-BYTES = 4 * K * T + E * K * N + E * (K // 32) * N + 4 * N * E + 4 * E * C + 2 * 128 * (E * C // 16) + 4 * N * T
+SLOTS = E * C
+
+P = 128
+PACK = 4
+PASSES = K // (P * PACK)
+BLOCKS = N // P
+LIST_ROWS = 16
+
+FLOPS = 2 * K * N * SLOTS
+BYTES = 4 * K * T + E * K * N + E * (K // 32) * N + 4 * N * E + 4 * SLOTS + 2 * P * (SLOTS // LIST_ROWS) + 4 * N * T
 
 F32 = mybir.dt.float32
 BF16 = mybir.dt.bfloat16
@@ -13,24 +21,20 @@ U32 = mybir.dt.uint32
 U16 = mybir.dt.uint16
 U8 = mybir.dt.uint8
 FP8X4 = mybir.dt.float8_e4m3fn_x4
-ADD, MULT = mybir.AluOpType.add, mybir.AluOpType.mult
+IDENTITY = mybir.ActivationFunctionType.Identity
+MULT = mybir.AluOpType.mult
 
-P = 128
-PASSES = K // 512
-BLOCKS = N // P
-SLOTS = E * C
 WINDOW = 1024
-LOADS = (((0, 256), (256, 512)), ((0, 768),), ((0, 768),), ((0, 512), (512, 256)))
-COPIES = (
-    ((0, 128, "s"), (128, 128, "v"), (256, 384, "s"), (640, 128, "v")),
-    ((0, 640, "s"), (640, 128, "v")),
-    ((0, 640, "s"), (640, 128, "v")),
-    ((0, 256, "s"), (256, 256, "s"), (512, 256, "v")),
-)
-PIECES = ((0, 384), (384, 384))
-GROUPS = ((0, 1), (1, 3), (3, 5), (5, 6))
-SCALE_LOADS = ((0, 1), (1, 3), (3, 6))
-QUANTS = (((0, 256), (256, 512)), ((0, 512), (512, 256)), ((0, 512), (512, 256)), ((0, 256), (256, 256), (512, 256)))
+
+VECTOR_TOKENS = (384, 256, 256, 256)
+
+QUANTISED = ((512, 256), (0, 512))
+
+LAST_GATHERS = ((0, SLOTS // 2), (SLOTS // 2, SLOTS // 2))
+
+SCALE_RUNS = ((0, 1), (1, 3), (3, 6))
+
+SCATTER_GROUPS = ((0, 1), (1, 3), (3, 5), (5, 6))
 
 
 def tile_routed_moe_kernel(tc, xT, w_words, w_scales, b, gate, offs, out):
@@ -39,108 +43,97 @@ def tile_routed_moe_kernel(tc, xT, w_words, w_scales, b, gate, offs, out):
         keep = ctx.enter_context(tc.tile_pool(name="keep", bufs=1))
         psum = ctx.enter_context(tc.psum_pool(name="psum", bufs=8))
 
-        x_planes = xT.rearrange("(g p t) n -> g p t n", p=P, t=4)
-        raw = {}
-        offsets = keep.tile([P, SLOTS // 16], U16, name="offsets")
+        x_rows = xT.rearrange("(g p t) n -> g p t n", p=P, t=PACK)
+        x_raw = []
+        offsets = keep.tile([P, SLOTS // LIST_ROWS], U16, name="offsets")
         for g in range(PASSES):
-            for c0, width in LOADS[g]:
-                tile = keep.tile([P, 4, width], F32, name=f"raw_{g}_{c0}")
-                nc.sync.dma_start(tile[:], x_planes[g, :, :, c0 : c0 + width])
-                raw[g, c0] = tile
+            raw = keep.tile([P, PACK, T], F32, name=f"x_raw_{g}")
+            nc.sync.dma_start(raw[:], x_rows[g])
+            x_raw.append(raw)
             if g == 0:
                 nc.sync.dma_start(offsets[:], offs)
 
         bias = keep.tile([P, BLOCKS, E], F32, name="bias")
-        nc.scalar.dma_start(bias[:], b.rearrange("(c p) e -> p c e", p=P))
+        nc.sync.dma_start(bias[:], b.rearrange("(m p) e -> p m e", p=P))
 
         w_planes = []
-        for e0, e1 in SCALE_LOADS:
-            tile = keep.tile([P, (e1 - e0) * PASSES, N // 4], I32, name=f"w_plane_{e0}", align_bytes=64)
-            nc.vector.memset(tile[:], 0)
-            w_planes.append(tile)
-        plane = keep.tile([P, WINDOW], U8, name="plane", align_bytes=64)
-        nc.gpsimd.memset(plane[:], 0)
-        codes = []
+        for e0, e1 in SCALE_RUNS:
+            scale_words = keep.tile([P, (e1 - e0) * PASSES, N // 4], I32, name=f"w_scales_{e0}", align_bytes=64)
+            nc.vector.memset(scale_words[:], 0)
+            w_planes.append(scale_words)
+
+        token_scales = keep.tile([P, WINDOW], U8, name="token_scales", align_bytes=64)
+        nc.gpsimd.memset(token_scales[:], 0)
+        token_codes = []
         for g in range(PASSES):
-            tile = keep.tile([P, WINDOW], I32, name=f"codes_{g}", align_bytes=64)
-            nc.vector.memset(tile[:, T:], 0)
-            codes.append(tile)
+            words = keep.tile([P, WINDOW], I32, name=f"token_codes_{g}", align_bytes=64)
+            nc.vector.memset(words[:, T:], 0)
+            token_codes.append(words)
 
         gates = keep.tile([P, SLOTS], F32, name="gates")
         weights = []
-        w_bytes = []
-        for (e0, e1), tile in zip(SCALE_LOADS, w_planes):
+        weight_scales = []
+        for (e0, e1), scale_words in zip(SCALE_RUNS, w_planes):
+            scale_rows = w_scales[e0:e1].rearrange("e g (q i) n -> i q (e g) n", i=4)
             for i in range(4):
-                nc.sync.dma_start(
-                    tile[i:P:32, :, :],
-                    w_scales[e0:e1].rearrange("e a (q i) n -> i q (e a) n", i=4)[i].bitcast(I32),
-                )
+                nc.sync.dma_start(scale_words[i:P:32, :, :], scale_rows[i].bitcast(I32))
             for e in range(e0, e1):
-                w_bytes.append(tile[:].bitcast(U8)[:, (e - e0) * PASSES : (e - e0 + 1) * PASSES, :])
+                weight_scales.append(scale_words[:].bitcast(U8)[:, (e - e0) * PASSES : (e - e0 + 1) * PASSES, :])
                 words = keep.tile([P, PASSES, N], I32, name=f"weights_{e}", align_bytes=64)
-                nc.sync.dma_start(words[:], w_words[e].rearrange("a p n r -> p a (n r)").bitcast(I32))
+                nc.sync.dma_start(words[:], w_words[e].rearrange("g p n r -> p g (n r)").bitcast(I32))
                 weights.append(words)
                 if e == 0:
                     nc.sync.dma_start(gates[:], gate[0:P, :])
 
-        def source(g, c0, width):
-            for l0, lw in LOADS[g]:
-                if l0 <= c0 and c0 + width <= l0 + lw:
-                    return raw[g, l0][:, :, c0 - l0 : c0 - l0 + width]
-
         slot_codes = []
         for g in range(PASSES):
-            grouped = keep.tile([P, T, 4], BF16, name=f"grouped_{g}", align_bytes=64)
-            for c0, width, engine in COPIES[g]:
-                view = source(g, c0, width).rearrange("p t (c i) -> p c t i", i=4)
-                into = grouped[:, c0 : c0 + width, :].rearrange("p (c i) t -> p c t i", i=4)
-                if engine == "s":
-                    nc.scalar.copy(into, view)
-                else:
-                    nc.vector.tensor_copy(into, view)
-            for c0, width in QUANTS[g]:
+            grouped = keep.tile([P, T, PACK], BF16, name=f"grouped_{g}", align_bytes=64)
+            source = x_raw[g][:].rearrange("p t (c i) -> p c t i", i=4)
+            target = grouped[:].rearrange("p (c i) t -> p c t i", i=4)
+            split = (T - VECTOR_TOKENS[g]) // 4
+            nc.vector.tensor_copy(target[:, split:], source[:, split:])
+            nc.scalar.copy(target[:, :split], source[:, :split])
+            for t0, tokens in QUANTISED:
                 nc.vector.quantize_mx(
-                    out=codes[g][:, c0 : c0 + width].bitcast(FP8X4),
-                    scales=plane[4 * g : P, c0 : c0 + width],
-                    in_=grouped[:, c0 : c0 + width, :].rearrange("p n t -> p (n t)"),
+                    out=token_codes[g][:, t0 : t0 + tokens].bitcast(FP8X4),
+                    scales=token_scales[4 * g : P, t0 : t0 + tokens],
+                    in_=grouped[:, t0 : t0 + tokens, :].rearrange("p n t -> p (n t)"),
                 )
-            tile = keep.tile([P, SLOTS], U32, name=f"slot_codes_{g}", align_bytes=64)
+            words = keep.tile([P, SLOTS], U32, name=f"slot_codes_{g}", align_bytes=64)
             if g < PASSES - 1:
-                nc.vector.tensor_copy(tile[:], codes[g][:].bitcast(U32).indirect(offsets[:]))
-            slot_codes.append(tile)
-        slot_plane = keep.tile([P, SLOTS], U8, name="slot_plane", align_bytes=64)
-        for s0, n in PIECES:
-            here = slice(s0, s0 + n)
-            picked = offsets[:, s0 // 16 : (s0 + n) // 16]
-            nc.vector.tensor_copy(slot_codes[-1][:, here], codes[-1][:].bitcast(U32).indirect(picked))
-            nc.vector.tensor_copy(slot_plane[:, here], plane[:].indirect(picked))
+                nc.vector.tensor_copy(words[:], token_codes[g][:].bitcast(U32).indirect(offsets[:]))
+            slot_codes.append(words)
+        slot_scales = keep.tile([P, SLOTS], U8, name="slot_scales", align_bytes=64)
+        for s0, n in LAST_GATHERS:
+            slots = slice(s0, s0 + n)
+            picked = offsets[:, s0 // LIST_ROWS : (s0 + n) // LIST_ROWS]
+            nc.vector.tensor_copy(slot_codes[-1][:, slots], token_codes[-1][:].bitcast(U32).indirect(picked))
+            nc.vector.tensor_copy(slot_scales[:, slots], token_scales[:].indirect(picked))
 
-        placed = []
+        results = []
         for m in range(BLOCKS):
-            tile = keep.tile([P, T], F32, name=f"placed_{m}")
-            placed.append(tile)
-        for e0, e1 in GROUPS:
+            result = keep.tile([P, T], F32, name=f"result_{m}")
+            results.append(result)
+        for e0, e1 in SCATTER_GROUPS:
             slots = slice(e0 * C, e1 * C)
-            picked = offsets[:, e0 * C // 16 : e1 * C // 16]
+            picked = offsets[:, e0 * C // LIST_ROWS : e1 * C // LIST_ROWS]
             for m in range(BLOCKS):
+                features = slice(m * P, (m + 1) * P)
                 sums = psum.tile([P, 512], F32, name="sums")
-                rows = slice(m * P, (m + 1) * P)
                 y = keep.tile([P, (e1 - e0) * C], F32, name=f"y_{e0}_{m}")
                 for e in range(e0, e1):
-                    here = slice((e - e0) * C, (e - e0 + 1) * C)
+                    places = slice((e - e0) * C, (e - e0 + 1) * C)
                     for g in range(PASSES):
                         nc.tensor.matmul_mx(
-                            out=sums[:, here],
-                            lhsT=weights[e][:, g, rows].bitcast(FP8X4),
-                            lhsT_scale=w_bytes[e][:, g, rows],
+                            out=sums[:, places],
+                            lhsT=weights[e][:, g, features].bitcast(FP8X4),
+                            lhsT_scale=weight_scales[e][:, g, features],
                             rhs=slot_codes[g][:, e * C : (e + 1) * C].bitcast(FP8X4),
-                            rhs_scale=slot_plane[4 * g : P, e * C : (e + 1) * C],
+                            rhs_scale=slot_scales[4 * g : P, e * C : (e + 1) * C],
                             start=(g == 0),
                             stop=(g == PASSES - 1),
                         )
-                    nc.scalar.activation(y[:, here], sums[:, here], mybir.ActivationFunctionType.Identity, bias=bias[:, m, e : e + 1])
-                z = keep.tile([P, (e1 - e0) * C], F32, name=f"z_{e0}_{m}")
-                nc.gpsimd.tensor_tensor(z[:], y[:], gates[:, slots], MULT)
-                nc.vector.tensor_copy(placed[m][:].indirect(picked), z[:])
+                    nc.scalar.activation(y[:, places], sums[:, places], IDENTITY, bias=bias[:, m, e : e + 1])
+                nc.vector.tensor_tensor(results[m][:].indirect(picked), y[:], gates[:, slots], MULT)
         for m in range(BLOCKS):
-            nc.sync.dma_start(out[m * P : (m + 1) * P, :], placed[m][:])
+            nc.sync.dma_start(out[m * P : (m + 1) * P, :], results[m][:])

from contextlib import ExitStack

import concourse.mybir as mybir

K, T, E, C, N = 2048, 768, 6, 128, 384
SLOTS = E * C

P = 128
PACK = 4
PASSES = K // (P * PACK)
BLOCKS = N // P
LIST_ROWS = 16

FLOPS = 2 * K * N * SLOTS
BYTES = 4 * K * T + E * K * N + E * (K // 32) * N + 4 * N * E + 4 * SLOTS + 2 * P * (SLOTS // LIST_ROWS) + 4 * N * T

F32 = mybir.dt.float32
BF16 = mybir.dt.bfloat16
I32 = mybir.dt.int32
U32 = mybir.dt.uint32
U16 = mybir.dt.uint16
U8 = mybir.dt.uint8
FP8X4 = mybir.dt.float8_e4m3fn_x4
IDENTITY = mybir.ActivationFunctionType.Identity
MULT = mybir.AluOpType.mult

WINDOW = 1024

VECTOR_TOKENS = (384, 256, 256, 256)

QUANTISED = ((512, 256), (0, 512))

LAST_GATHERS = ((0, SLOTS // 2), (SLOTS // 2, SLOTS // 2))

SCALE_RUNS = ((0, 1), (1, 3), (3, 6))

SCATTER_GROUPS = ((0, 1), (1, 3), (3, 5), (5, 6))


def tile_routed_moe_kernel(tc, xT, w_words, w_scales, b, gate, offs, out):
    nc = tc.nc
    with ExitStack() as ctx:
        keep = ctx.enter_context(tc.tile_pool(name="keep", bufs=1))
        psum = ctx.enter_context(tc.psum_pool(name="psum", bufs=8))

        x_rows = xT.rearrange("(g p t) n -> g p t n", p=P, t=PACK)
        x_raw = []
        offsets = keep.tile([P, SLOTS // LIST_ROWS], U16, name="offsets")
        for g in range(PASSES):
            raw = keep.tile([P, PACK, T], F32, name=f"x_raw_{g}")
            nc.sync.dma_start(raw[:], x_rows[g])
            x_raw.append(raw)
            if g == 0:
                nc.sync.dma_start(offsets[:], offs)

        bias = keep.tile([P, BLOCKS, E], F32, name="bias")
        nc.sync.dma_start(bias[:], b.rearrange("(m p) e -> p m e", p=P))

        w_planes = []
        for e0, e1 in SCALE_RUNS:
            scale_words = keep.tile([P, (e1 - e0) * PASSES, N // 4], I32, name=f"w_scales_{e0}", align_bytes=64)
            nc.vector.memset(scale_words[:], 0)
            w_planes.append(scale_words)

        token_scales = keep.tile([P, WINDOW], U8, name="token_scales", align_bytes=64)
        nc.gpsimd.memset(token_scales[:], 0)
        token_codes = []
        for g in range(PASSES):
            words = keep.tile([P, WINDOW], I32, name=f"token_codes_{g}", align_bytes=64)
            nc.vector.memset(words[:, T:], 0)
            token_codes.append(words)

        gates = keep.tile([P, SLOTS], F32, name="gates")
        weights = []
        weight_scales = []
        for (e0, e1), scale_words in zip(SCALE_RUNS, w_planes):
            scale_rows = w_scales[e0:e1].rearrange("e g (q i) n -> i q (e g) n", i=4)
            for i in range(4):
                nc.sync.dma_start(scale_words[i:P:32, :, :], scale_rows[i].bitcast(I32))
            for e in range(e0, e1):
                weight_scales.append(scale_words[:].bitcast(U8)[:, (e - e0) * PASSES : (e - e0 + 1) * PASSES, :])
                words = keep.tile([P, PASSES, N], I32, name=f"weights_{e}", align_bytes=64)
                nc.sync.dma_start(words[:], w_words[e].rearrange("g p n r -> p g (n r)").bitcast(I32))
                weights.append(words)
                if e == 0:
                    nc.sync.dma_start(gates[:], gate[0:P, :])

        slot_codes = []
        for g in range(PASSES):
            grouped = keep.tile([P, T, PACK], BF16, name=f"grouped_{g}", align_bytes=64)
            source = x_raw[g][:].rearrange("p t (c i) -> p c t i", i=4)
            target = grouped[:].rearrange("p (c i) t -> p c t i", i=4)
            split = (T - VECTOR_TOKENS[g]) // 4
            nc.vector.tensor_copy(target[:, split:], source[:, split:])
            nc.scalar.copy(target[:, :split], source[:, :split])
            for t0, tokens in QUANTISED:
                nc.vector.quantize_mx(
                    out=token_codes[g][:, t0 : t0 + tokens].bitcast(FP8X4),
                    scales=token_scales[4 * g : P, t0 : t0 + tokens],
                    in_=grouped[:, t0 : t0 + tokens, :].rearrange("p n t -> p (n t)"),
                )
            words = keep.tile([P, SLOTS], U32, name=f"slot_codes_{g}", align_bytes=64)
            if g < PASSES - 1:
                nc.vector.tensor_copy(words[:], token_codes[g][:].bitcast(U32).indirect(offsets[:]))
            slot_codes.append(words)
        slot_scales = keep.tile([P, SLOTS], U8, name="slot_scales", align_bytes=64)
        for s0, n in LAST_GATHERS:
            slots = slice(s0, s0 + n)
            picked = offsets[:, s0 // LIST_ROWS : (s0 + n) // LIST_ROWS]
            nc.vector.tensor_copy(slot_codes[-1][:, slots], token_codes[-1][:].bitcast(U32).indirect(picked))
            nc.vector.tensor_copy(slot_scales[:, slots], token_scales[:].indirect(picked))

        results = []
        for m in range(BLOCKS):
            result = keep.tile([P, T], F32, name=f"result_{m}")
            results.append(result)
        for e0, e1 in SCATTER_GROUPS:
            slots = slice(e0 * C, e1 * C)
            picked = offsets[:, e0 * C // LIST_ROWS : e1 * C // LIST_ROWS]
            for m in range(BLOCKS):
                features = slice(m * P, (m + 1) * P)
                sums = psum.tile([P, 512], F32, name="sums")
                y = keep.tile([P, (e1 - e0) * C], F32, name=f"y_{e0}_{m}")
                for e in range(e0, e1):
                    places = slice((e - e0) * C, (e - e0 + 1) * C)
                    for g in range(PASSES):
                        nc.tensor.matmul_mx(
                            out=sums[:, places],
                            lhsT=weights[e][:, g, features].bitcast(FP8X4),
                            lhsT_scale=weight_scales[e][:, g, features],
                            rhs=slot_codes[g][:, e * C : (e + 1) * C].bitcast(FP8X4),
                            rhs_scale=slot_scales[4 * g : P, e * C : (e + 1) * C],
                            start=(g == 0),
                            stop=(g == PASSES - 1),
                        )
                    nc.scalar.activation(y[:, places], sums[:, places], IDENTITY, bias=bias[:, m, e : e + 1])
                nc.vector.tensor_tensor(results[m][:].indirect(picked), y[:], gates[:, slots], MULT)
        for m in range(BLOCKS):
            nc.sync.dma_start(out[m * P : (m + 1) * P, :], results[m][:])
